import numpy as np
import ml_dtypes


def mxq(x, axis, fmt="e4m3"):
    dtype, down = {"e4m3": (ml_dtypes.float8_e4m3fn, 7), "e5m2": (ml_dtypes.float8_e5m2, 14)}[fmt]
    v = np.moveaxis(np.asarray(x, np.float32).astype(ml_dtypes.bfloat16).astype(np.float64), axis, -1)
    blocks = v.reshape(v.shape[:-1] + (-1, 32))
    amax = np.abs(blocks).max(-1, keepdims=True)
    byte = np.maximum(np.where(amax > 0, np.frexp(amax)[1] - 1 + 127, 0) - down, 1)
    scale = np.exp2(byte - 127.0)
    codes = (blocks / scale).astype(np.float32).astype(dtype).astype(np.float64)
    return np.moveaxis((codes * scale).reshape(v.shape), -1, axis)


WIDE = False


def mx_kscale(k):
    if not WIDE:
        return np.ones(k)
    levels = np.array([10, -10, 5, -5, 0])
    if k % 512:
        return np.exp2(np.random.permutation(np.resize(levels, k // 32))).repeat(32)
    a = np.empty((k // 512, 16))
    for p in range(k // 512):
        a[p, :8] = np.random.permutation(np.resize(levels, 8))
        for g in range(8):
            far = levels[np.abs(levels - a[p, g]) >= 10]
            a[p, g + 8] = far[np.random.randint(len(far))]
    return np.exp2(a.ravel()).repeat(32)


def f64(x):
    return np.asarray(x).astype(np.float64)


def striped8(idx):
    return np.concatenate([v.reshape(-1, 16).T for v in idx]).astype(np.uint16)


def unstriped8(offs):
    return np.stack([offs[16 * g:16 * g + 16].T.reshape(-1) for g in range(8)]).astype(np.int64)


E2M1 = np.array([0.0, 0.5, 1.0, 1.5, 2.0, 3.0, 4.0, 6.0, -0.0, -0.5, -1.0, -1.5, -2.0, -3.0, -4.0, -6.0])


def pack_weight(w, fmt):
    k, n = w.shape
    w = f64(np.asarray(w, np.float32).astype(ml_dtypes.bfloat16)).reshape(k // 32, 32, n)
    amax = np.abs(w).max(1)
    if fmt == "e4m3":
        byte = np.frexp(amax)[1] - 1 + 127 - 7
    else:
        mant, ex = np.frexp(amax / 6.0)
        byte = np.where(mant > 0.5, ex, ex - 1) + 127
    byte = np.clip(np.where(amax > 0, byte, 1), 1, 254)
    scaled = (w * np.exp2(127.0 - byte)[:, None, :]).reshape(k, n).astype(np.float32)
    by_word = np.ascontiguousarray(scaled.reshape(k // 512, 128, 4, n).transpose(0, 1, 3, 2))
    if fmt == "e4m3":
        words = by_word.astype(ml_dtypes.float8_e4m3fn).view(np.uint8)
    else:
        c = by_word.astype(ml_dtypes.float4_e2m1fn).view(np.uint8) & 0xF
        words = (c[..., 0::2] | (c[..., 1::2] << 4)).reshape(k // 512, 128, 2 * n)
    return np.ascontiguousarray(words), np.ascontiguousarray(byte.astype(np.uint8).reshape(k // 512, 16, n))


def unpack_weight(words, scales, fmt):
    g, _, n = scales.shape
    words = np.ascontiguousarray(words).reshape(g, 128, n, -1)
    if fmt == "e4m3":
        vals = words.view(ml_dtypes.float8_e4m3fn).astype(np.float64)
    else:
        nib = np.empty((g, 128, n, 4), np.uint8)
        nib[..., 0::2] = words & 0xF
        nib[..., 1::2] = words >> 4
        vals = E2M1[nib]
    vals = vals * np.repeat(np.exp2(scales.astype(np.float64) - 127.0), 8, axis=1)[..., None]
    return vals.transpose(0, 1, 3, 2).reshape(g * 512, n)


K, M, T, S = 512, 256, 4096, 2048


def setup_inputs():
    n = np.random.standard_normal
    s = mx_kscale(K)[:, None]
    s2 = mx_kscale(512)[:, None]
    p_w4 = pack_weight(n((K, M)) / np.sqrt(K) / s, "e2m1")
    return {
        "x": (n((K, S)) * s).astype(np.float32),
        "w4_words": p_w4[0],
        "w4_scales": p_w4[1],
        "c": (n((512, S)) * s2).astype(np.float32),
        "u": (n((512, M)) / np.sqrt(512) / s2).astype(np.float32),
        "b": (0.3 * n(256)).astype(np.float32),
        "wgo": np.repeat(np.random.uniform(0.5, 2.0, (8, S)), 16, axis=0).astype(np.float32),
        "offs": striped8(np.stack([np.random.permutation(T)[:S] for _ in range(8)])),
    }


def reference(x, w4_words, w4_scales, c, u, b, wgo, offs):
    x_ = mxq(f64(x), 0, "e4m3")
    w4_ = unpack_weight(w4_words, w4_scales, "e2m1")
    c_ = mxq(f64(c), 0, "e4m3")
    u_ = mxq(f64(u), 0, "e4m3")
    y = w4_.T @ x_ + u_.T @ c_
    place = unstriped8(offs)[np.arange(M) % 128 // 16]
    out = np.zeros((M, T))
    out[np.arange(M)[:, None], place] = f64(wgo)[np.arange(M) % 128] * (y + f64(b)[:, None])
    return out

@@ -1,0 +1,130 @@
+from contextlib import ExitStack
+
+import concourse.mybir as mybir
+
+K, M, T, S = 512, 256, 4096, 2048
+FLOPS = 2 * 2 * K * M * S
+
+F32 = mybir.dt.float32
+BF16 = mybir.dt.bfloat16
+I32 = mybir.dt.int32
+U32 = mybir.dt.uint32
+U16 = mybir.dt.uint16
+U8 = mybir.dt.uint8
+FP8X4 = mybir.dt.float8_e4m3fn_x4
+FP4X4 = mybir.dt.float4_e2m1fn_x4
+MULT = mybir.AluOpType.mult
+IDENT = mybir.ActivationFunctionType.Identity
+
+P = 128
+PACK = 4
+W = 256
+NCH = S // W
+LAGGED = 3
+WGO = {0: (0, 256), 1: (256, 768), 3: (768, 1280), 5: (1280, 2048)}
+
+
+def tile_list_hscat_d_bias_kernel(tc, x, w4_words, w4_scales, c, u, b, wgo, offs, out):
+    nc = tc.nc
+    with ExitStack() as ctx:
+        keep = ctx.enter_context(tc.tile_pool(name="keep", bufs=1))
+        psum = ctx.enter_context(tc.psum_pool(name="psum", bufs=4))
+
+        offsets = keep.tile([P, S // 16], U16, name="offsets")
+        w_words = keep.tile([P, 2 * M], U8, name="w_words", align_bytes=64)
+        w_scales = keep.tile([P, M], U8, name="w_scales", align_bytes=64)
+        bias = keep.tile([P, 2], F32, name="bias")
+        weights = keep.tile([P, S], F32, name="weights")
+        pages = [keep.tile([P, T], F32, name="page%d" % h) for h in range(2)]
+        y_last = keep.tile([P, LAGGED * W], F32, name="y_last")
+
+        def load(src, a, e, name):
+            raw = keep.tile([P, PACK, e - a], F32, name="raw_" + name)
+            nc.sync.dma_start(out=raw[:], in_=src[:, a:e].rearrange("(p t) w -> p t w", t=PACK))
+            return raw
+
+        def first_copy(out, in_):
+            nc.scalar.activation(out=out, in_=in_, func=IDENT)
+
+        def cast(engine_copy, raw, name):
+            width = raw.shape[2]
+            grouped = keep.tile([P, width * PACK], BF16, name="bf_" + name, align_bytes=64)
+            engine_copy(
+                out=grouped[:].rearrange("p (w i t) -> p w t i", i=4, t=PACK),
+                in_=raw[:].rearrange("p t (w i) -> p w t i", i=4),
+            )
+            return grouped
+
+        def quantize(grouped, name):
+            width = grouped.shape[1] // PACK
+            codes = keep.tile([P, width], U32, name="codes_" + name, align_bytes=64)
+            scales = keep.tile([P, width], U8, name="scales_" + name, align_bytes=64)
+            nc.vector.quantize_mx(out=codes[:].bitcast(FP8X4), scales=scales[:], in_=grouped[:])
+            return codes, scales
+
+        def multiply(h, uq, cq, xq):
+            acc = psum.tile([P, W], F32, name="acc%d" % h)
+            rows = slice(P * h, P * (h + 1))
+            nc.tensor.matmul_mx(
+                out=acc[:], lhsT=uq[0][:, rows].bitcast(FP8X4), lhsT_scale=uq[1][:, rows],
+                rhs=cq[0][:].bitcast(FP8X4), rhs_scale=cq[1][:], start=True, stop=False)
+            for a in range(0, W, P):
+                nc.tensor.matmul_mx(
+                    out=acc[:, a:a + P], lhsT=w_words[:, 2 * P * h:2 * P * (h + 1)].bitcast(FP4X4),
+                    lhsT_scale=w_scales[:, rows],
+                    rhs=xq[0][:, a:a + P].bitcast(FP8X4), rhs_scale=xq[1][:, a:a + P],
+                    start=False, stop=(a + P == W))
+            return acc
+
+        def drain(h, acc, y):
+            nc.scalar.activation(out=y, in_=acc[:], func=IDENT, bias=bias[:, h:h + 1])
+
+        def place(h, y, a, e):
+            nc.vector.tensor_tensor(pages[h][:].indirect(offsets[:, a // 16:e // 16]), y, weights[:, a:e], MULT)
+
+        nc.vector.memset(w_scales[:].bitcast(I32), 0)
+        nc.vector.memset(pages[0][:, 0:1], 0.0)
+        nc.vector.memset(pages[0][:, 1:T], 0.0)
+        nc.gpsimd.memset(pages[1][:], 0.0)
+
+        raw_u = load(u, 0, M, "u")
+        raw_c = []
+        raw_x = []
+        for i in range(NCH):
+            raw_c.append(load(c, i * W, (i + 1) * W, "c%d" % i))
+            raw_x.append(load(x, i * W, (i + 1) * W, "x%d" % i))
+            if i == 0:
+                nc.scalar.dma_start(out=w_words[:].bitcast(I32), in_=w4_words[0].bitcast(I32))
+                for q in range(4):
+                    nc.scalar.dma_start(out=w_scales[32 * q:32 * q + 4, :].bitcast(I32),
+                                        in_=w4_scales[0, 4 * q:4 * q + 4, :].bitcast(I32))
+                with nc.allow_non_contiguous_dma(reason="one bias value a partition"):
+                    nc.sync.dma_start(out=bias[:], in_=b.rearrange("(h p) -> p h", p=P))
+                nc.sync.dma_start(offsets[:], offs)
+            if i in WGO:
+                nc.sync.dma_start(out=weights[:, WGO[i][0]:WGO[i][1]], in_=wgo[:, WGO[i][0]:WGO[i][1]])
+
+        uq = quantize(cast(first_copy, raw_u, "u"), "u")
+        first_late = NCH - LAGGED
+        accs = []
+        for i in range(NCH):
+            cq = quantize(cast(nc.scalar.copy, raw_c[i], "c%d" % i), "c%d" % i)
+            if 2 <= i - 1 < first_late:
+                drain(0, accs[i - 1][0], raw_c[i][:, 0, :])
+                place(0, raw_c[i][:, 0, :], (i - 1) * W, i * W)
+            xq = quantize(cast(nc.vector.tensor_copy if i == 0 else nc.scalar.copy, raw_x[i], "x%d" % i), "x%d" % i)
+            if i >= 1:
+                h = 1 if i - 1 < first_late else 0
+                drain(h, accs[i - 1][h], raw_x[i][:, 0, :])
+                place(h, raw_x[i][:, 0, :], (i - 1) * W, i * W)
+            accs.append([multiply(h, uq, cq, xq) for h in range(2)])
+            if i < 2 or i == NCH - 1:
+                drain(0, accs[i][0], raw_c[i][:, 0, :])
+                place(0, raw_c[i][:, 0, :], i * W, (i + 1) * W)
+        for s in range(0, T, 2048):
+            nc.sync.dma_start(out=out[0:P, s:s + 2048], in_=pages[0][:, s:s + 2048])
+        for i in range(first_late, NCH):
+            drain(1, accs[i][1], y_last[:, (i - first_late) * W:(i - first_late + 1) * W])
+        place(1, y_last[:], first_late * W, S)
+        for s in range(0, T, 2048):
+            nc.sync.dma_start(out=out[P:2 * P, s:s + 2048], in_=pages[1][:, s:s + 2048])

@@ -21,7 +21,9 @@ PACK = 4
 W = 256
 NCH = S // W
 LAGGED = 3
-WGO = {0: (0, 256), 1: (256, 768), 3: (768, 1280), 5: (1280, 2048)}
+LOADS = [("c", 0, 1), ("x", 0, 1), ("small", 0, 0), ("w", 0, 1), ("c", 1, 2), ("x", 1, 2), ("w", 1, 2),
+         ("c", 2, 3), ("x", 2, 3), ("w", 2, 4), ("c", 3, 5), ("x", 3, 4), ("x", 4, 6), ("w", 4, 6),
+         ("c", 5, 7), ("x", 6, 8), ("w", 6, 8), ("c", 7, 8)]
 
 
 def tile_list_hscat_d_bias_kernel(tc, x, w4_words, w4_scales, c, u, b, wgo, offs, out):
@@ -51,7 +53,7 @@ def tile_list_hscat_d_bias_kernel(tc, x, w4_words, w4_scales, c, u, b, wgo, offs
             grouped = keep.tile([P, width * PACK], BF16, name="bf_" + name, align_bytes=64)
             engine_copy(
                 out=grouped[:].rearrange("p (w i t) -> p w t i", i=4, t=PACK),
-                in_=raw[:].rearrange("p t (w i) -> p w t i", i=4),
+                in_=raw.rearrange("p t (w i) -> p w t i", i=4),
             )
             return grouped
 
@@ -82,29 +84,31 @@ def tile_list_hscat_d_bias_kernel(tc, x, w4_words, w4_scales, c, u, b, wgo, offs
         def place(h, y, a, e):
             nc.vector.tensor_tensor(pages[h][:].indirect(offsets[:, a // 16:e // 16]), y, weights[:, a:e], MULT)
 
-        nc.vector.memset(w_scales[:].bitcast(I32), 0)
+        nc.gpsimd.memset(w_scales[:].bitcast(I32), 0)
         nc.vector.memset(pages[0][:, 0:1], 0.0)
         nc.vector.memset(pages[0][:, 1:T], 0.0)
         nc.gpsimd.memset(pages[1][:], 0.0)
 
         raw_u = load(u, 0, M, "u")
+        nc.sync.dma_start(out=w_words[:].bitcast(I32), in_=w4_words[0].bitcast(I32))
+        for q in range(4):
+            nc.sync.dma_start(out=w_scales[32 * q:32 * q + 4, :].bitcast(I32),
+                              in_=w4_scales[0, 4 * q:4 * q + 4, :].bitcast(I32))
         raw_c = []
         raw_x = []
-        for i in range(NCH):
-            raw_c.append(load(c, i * W, (i + 1) * W, "c%d" % i))
-            raw_x.append(load(x, i * W, (i + 1) * W, "x%d" % i))
-            if i == 0:
-                nc.scalar.dma_start(out=w_words[:].bitcast(I32), in_=w4_words[0].bitcast(I32))
-                for q in range(4):
-                    nc.scalar.dma_start(out=w_scales[32 * q:32 * q + 4, :].bitcast(I32),
-                                        in_=w4_scales[0, 4 * q:4 * q + 4, :].bitcast(I32))
+        for kind, a, e in LOADS:
+            if kind == "small":
+                nc.sync.dma_start(offsets[:], offs)
                 with nc.allow_non_contiguous_dma(reason="one bias value a partition"):
                     nc.sync.dma_start(out=bias[:], in_=b.rearrange("(h p) -> p h", p=P))
-                nc.sync.dma_start(offsets[:], offs)
-            if i in WGO:
-                nc.sync.dma_start(out=weights[:, WGO[i][0]:WGO[i][1]], in_=wgo[:, WGO[i][0]:WGO[i][1]])
+            elif kind == "w":
+                nc.sync.dma_start(out=weights[:, a * W:e * W], in_=wgo[:, a * W:e * W])
+            else:
+                raw = load(c if kind == "c" else x, a * W, e * W, "%s%d" % (kind, a))
+                for i in range(e - a):
+                    (raw_c if kind == "c" else raw_x).append(raw[:, :, i * W:(i + 1) * W])
 
-        uq = quantize(cast(first_copy, raw_u, "u"), "u")
+        uq = quantize(cast(first_copy, raw_u[:], "u"), "u")
         first_late = NCH - LAGGED
         accs = []
         for i in range(NCH):

from contextlib import ExitStack

import concourse.mybir as mybir

K, M, T, S = 512, 256, 4096, 2048
FLOPS = 2 * 2 * K * M * S

F32 = mybir.dt.float32
BF16 = mybir.dt.bfloat16
I32 = mybir.dt.int32
U32 = mybir.dt.uint32
U16 = mybir.dt.uint16
U8 = mybir.dt.uint8
FP8X4 = mybir.dt.float8_e4m3fn_x4
FP4X4 = mybir.dt.float4_e2m1fn_x4
MULT = mybir.AluOpType.mult
IDENT = mybir.ActivationFunctionType.Identity

P = 128
PACK = 4
W = 256
NCH = S // W
LAGGED = 3
LOADS = [("c", 0, 1), ("x", 0, 1), ("small", 0, 0), ("w", 0, 1), ("c", 1, 2), ("x", 1, 2), ("w", 1, 2),
         ("c", 2, 3), ("x", 2, 3), ("w", 2, 4), ("c", 3, 5), ("x", 3, 4), ("x", 4, 6), ("w", 4, 6),
         ("c", 5, 7), ("x", 6, 8), ("w", 6, 8), ("c", 7, 8)]


def tile_list_hscat_d_bias_kernel(tc, x, w4_words, w4_scales, c, u, b, wgo, offs, out):
    nc = tc.nc
    with ExitStack() as ctx:
        keep = ctx.enter_context(tc.tile_pool(name="keep", bufs=1))
        psum = ctx.enter_context(tc.psum_pool(name="psum", bufs=4))

        offsets = keep.tile([P, S // 16], U16, name="offsets")
        w_words = keep.tile([P, 2 * M], U8, name="w_words", align_bytes=64)
        w_scales = keep.tile([P, M], U8, name="w_scales", align_bytes=64)
        bias = keep.tile([P, 2], F32, name="bias")
        weights = keep.tile([P, S], F32, name="weights")
        pages = [keep.tile([P, T], F32, name="page%d" % h) for h in range(2)]
        y_last = keep.tile([P, LAGGED * W], F32, name="y_last")

        def load(src, a, e, name):
            raw = keep.tile([P, PACK, e - a], F32, name="raw_" + name)
            nc.sync.dma_start(out=raw[:], in_=src[:, a:e].rearrange("(p t) w -> p t w", t=PACK))
            return raw

        def first_copy(out, in_):
            nc.scalar.activation(out=out, in_=in_, func=IDENT)

        def cast(engine_copy, raw, name):
            width = raw.shape[2]
            grouped = keep.tile([P, width * PACK], BF16, name="bf_" + name, align_bytes=64)
            engine_copy(
                out=grouped[:].rearrange("p (w i t) -> p w t i", i=4, t=PACK),
                in_=raw.rearrange("p t (w i) -> p w t i", i=4),
            )
            return grouped

        def quantize(grouped, name):
            width = grouped.shape[1] // PACK
            codes = keep.tile([P, width], U32, name="codes_" + name, align_bytes=64)
            scales = keep.tile([P, width], U8, name="scales_" + name, align_bytes=64)
            nc.vector.quantize_mx(out=codes[:].bitcast(FP8X4), scales=scales[:], in_=grouped[:])
            return codes, scales

        def multiply(h, uq, cq, xq):
            acc = psum.tile([P, W], F32, name="acc%d" % h)
            rows = slice(P * h, P * (h + 1))
            nc.tensor.matmul_mx(
                out=acc[:], lhsT=uq[0][:, rows].bitcast(FP8X4), lhsT_scale=uq[1][:, rows],
                rhs=cq[0][:].bitcast(FP8X4), rhs_scale=cq[1][:], start=True, stop=False)
            for a in range(0, W, P):
                nc.tensor.matmul_mx(
                    out=acc[:, a:a + P], lhsT=w_words[:, 2 * P * h:2 * P * (h + 1)].bitcast(FP4X4),
                    lhsT_scale=w_scales[:, rows],
                    rhs=xq[0][:, a:a + P].bitcast(FP8X4), rhs_scale=xq[1][:, a:a + P],
                    start=False, stop=(a + P == W))
            return acc

        def drain(h, acc, y):
            nc.scalar.activation(out=y, in_=acc[:], func=IDENT, bias=bias[:, h:h + 1])

        def place(h, y, a, e):
            nc.vector.tensor_tensor(pages[h][:].indirect(offsets[:, a // 16:e // 16]), y, weights[:, a:e], MULT)

        nc.gpsimd.memset(w_scales[:].bitcast(I32), 0)
        nc.vector.memset(pages[0][:, 0:1], 0.0)
        nc.vector.memset(pages[0][:, 1:T], 0.0)
        nc.gpsimd.memset(pages[1][:], 0.0)

        raw_u = load(u, 0, M, "u")
        nc.sync.dma_start(out=w_words[:].bitcast(I32), in_=w4_words[0].bitcast(I32))
        for q in range(4):
            nc.sync.dma_start(out=w_scales[32 * q:32 * q + 4, :].bitcast(I32),
                              in_=w4_scales[0, 4 * q:4 * q + 4, :].bitcast(I32))
        raw_c = []
        raw_x = []
        for kind, a, e in LOADS:
            if kind == "small":
                nc.sync.dma_start(offsets[:], offs)
                with nc.allow_non_contiguous_dma(reason="one bias value a partition"):
                    nc.sync.dma_start(out=bias[:], in_=b.rearrange("(h p) -> p h", p=P))
            elif kind == "w":
                nc.sync.dma_start(out=weights[:, a * W:e * W], in_=wgo[:, a * W:e * W])
            else:
                raw = load(c if kind == "c" else x, a * W, e * W, "%s%d" % (kind, a))
                for i in range(e - a):
                    (raw_c if kind == "c" else raw_x).append(raw[:, :, i * W:(i + 1) * W])

        uq = quantize(cast(first_copy, raw_u[:], "u"), "u")
        first_late = NCH - LAGGED
        accs = []
        for i in range(NCH):
            cq = quantize(cast(nc.scalar.copy, raw_c[i], "c%d" % i), "c%d" % i)
            if 2 <= i - 1 < first_late:
                drain(0, accs[i - 1][0], raw_c[i][:, 0, :])
                place(0, raw_c[i][:, 0, :], (i - 1) * W, i * W)
            xq = quantize(cast(nc.vector.tensor_copy if i == 0 else nc.scalar.copy, raw_x[i], "x%d" % i), "x%d" % i)
            if i >= 1:
                h = 1 if i - 1 < first_late else 0
                drain(h, accs[i - 1][h], raw_x[i][:, 0, :])
                place(h, raw_x[i][:, 0, :], (i - 1) * W, i * W)
            accs.append([multiply(h, uq, cq, xq) for h in range(2)])
            if i < 2 or i == NCH - 1:
                drain(0, accs[i][0], raw_c[i][:, 0, :])
                place(0, raw_c[i][:, 0, :], i * W, (i + 1) * W)
        for s in range(0, T, 2048):
            nc.sync.dma_start(out=out[0:P, s:s + 2048], in_=pages[0][:, s:s + 2048])
        for i in range(first_late, NCH):
            drain(1, accs[i][1], y_last[:, (i - first_late) * W:(i - first_late + 1) * W])
        place(1, y_last[:], first_late * W, S)
        for s in range(0, T, 2048):
            nc.sync.dma_start(out=out[P:2 * P, s:s + 2048], in_=pages[1][:, s:s + 2048])
